import numpy as np
import ml_dtypes


def mxq(x, axis, fmt="e4m3"):
    dtype, down = {"e4m3": (ml_dtypes.float8_e4m3fn, 7), "e5m2": (ml_dtypes.float8_e5m2, 14)}[fmt]
    v = np.moveaxis(np.asarray(x, np.float32).astype(ml_dtypes.bfloat16).astype(np.float64), axis, -1)
    blocks = v.reshape(v.shape[:-1] + (-1, 32))
    amax = np.abs(blocks).max(-1, keepdims=True)
    byte = np.maximum(np.where(amax > 0, np.frexp(amax)[1] - 1 + 127, 0) - down, 1)
    scale = np.exp2(byte - 127.0)
    codes = (blocks / scale).astype(np.float32).astype(dtype).astype(np.float64)
    return np.moveaxis((codes * scale).reshape(v.shape), -1, axis)


WIDE = False


def mx_kscale(k, group=512):
    if not WIDE:
        return np.ones(k)
    levels = np.array([10, -10, 5, -5, 0])
    if group != 512:
        return np.exp2(np.random.permutation(np.resize(levels, k // group))).repeat(group)
    if k % 512:
        return np.exp2(np.random.permutation(np.resize(levels, k // 32))).repeat(32)
    a = np.empty((k // 512, 16))
    for p in range(k // 512):
        a[p, :8] = np.random.permutation(np.resize(levels, 8))
        for g in range(8):
            far = levels[np.abs(levels - a[p, g]) >= 10]
            a[p, g + 8] = far[np.random.randint(len(far))]
    return np.exp2(a.ravel()).repeat(32)


def f64(x):
    return np.asarray(x).astype(np.float64)


E2M1 = np.array([0.0, 0.5, 1.0, 1.5, 2.0, 3.0, 4.0, 6.0, -0.0, -0.5, -1.0, -1.5, -2.0, -3.0, -4.0, -6.0])


def pack_group(w):
    k, n = w.shape
    w = f64(np.asarray(w, np.float32).astype(ml_dtypes.bfloat16)).reshape(k // 32, 32, n)
    amax = np.abs(w).max(1)
    mant, ex = np.frexp(amax / 6.0)
    byte = np.clip(np.where(amax > 0, np.where(mant > 0.5, ex, ex - 1) + 127, 1), 1, 254)
    scaled = (w * np.exp2(127.0 - byte)[:, None, :]).reshape(k, n).astype(np.float32)
    c = np.ascontiguousarray(scaled.reshape(k // 4, 4, n).transpose(0, 2, 1)).astype(ml_dtypes.float4_e2m1fn).view(np.uint8) & 0xF
    return np.ascontiguousarray((c[..., 0::2] | (c[..., 1::2] << 4)).reshape(k // 4, 2 * n)), byte.astype(np.uint8)


def unpack_group(words, scales):
    p, n = words.shape[0], scales.shape[1]
    words = np.ascontiguousarray(words).reshape(p, n, 2)
    nib = np.empty((p, n, 4), np.uint8)
    nib[..., 0::2] = words & 0xF
    nib[..., 1::2] = words >> 4
    return E2M1[nib].transpose(0, 2, 1).reshape(4 * p, n) * np.repeat(np.exp2(scales.astype(np.float64) - 127.0), 32, axis=0)


def sigmoid(v):
    return 1.0 / (1.0 + np.exp(-v))


G, D, M, O, N = 2, 256, 256, 256, 512


def setup_inputs():
    n = np.random.standard_normal
    s_d = mx_kscale(D, 0)
    s_o = mx_kscale(O, 0)
    w1_ = [pack_group(w) for w in n((G, D, M)) / np.sqrt(D) / s_d[:, None]]
    w2_ = [pack_group(w) for w in n((G, D, M)) / np.sqrt(D) / s_d[:, None]]
    wo_ = [pack_group(w) for w in n((G, O, M)) / np.sqrt(O) / s_o[:, None]]
    return {
        "x": (n((G, D, N)) * s_d[:, None]).astype(np.float32),
        "w1_words": np.stack([w[0] for w in w1_]),
        "w1_scales": np.stack([w[1] for w in w1_]),
        "w2_words": np.stack([w[0] for w in w2_]),
        "w2_scales": np.stack([w[1] for w in w2_]),
        "tp": (np.random.uniform(0.5, 1.2, (G, M, 1))).astype(np.float32),
        "wo_words": np.stack([w[0] for w in wo_]),
        "wo_scales": np.stack([w[1] for w in wo_]),
        "dy": (n((G, O, N)) * s_o[:, None]).astype(np.float32),
        "old": (0.3 * n((G, M, N))).astype(np.float32),
    }


def reference(x, w1_words, w1_scales, w2_words, w2_scales, tp, wo_words, wo_scales, dy, old):
    w1 = np.stack([unpack_group(w1_words[g], w1_scales[g]) for g in range(G)])
    xq = mxq(f64(x), 1, "e4m3")
    z1 = w1.transpose(0, 2, 1) @ xq
    w2 = np.stack([unpack_group(w2_words[g], w2_scales[g]) for g in range(G)])
    z2 = w2.transpose(0, 2, 1) @ xq
    s1 = z1 * f64(tp)
    wo = np.stack([unpack_group(wo_words[g], wo_scales[g]) for g in range(G)])
    dyq = mxq(f64(dy), 1, "e4m3")
    c0 = wo.transpose(0, 2, 1) @ dyq
    dls = np.sum(c0 * sigmoid(z2) * (-1.0), axis=-1, keepdims=True)
    ds1 = c0 * sigmoid(z2) + dls / np.sum(np.exp(s1), axis=-1, keepdims=True) * np.exp(s1)
    dz1 = ds1 * f64(tp)
    y = dz1 + f64(old)
    return y

@@ -1,0 +1,244 @@
+from contextlib import ExitStack
+
+import concourse.mybir as mybir
+
+G, D, M, N = 2, 256, 256, 512
+FLOPS = 3 * 2 * G * D * M * N
+
+F32 = mybir.dt.float32
+BF16 = mybir.dt.bfloat16
+I32 = mybir.dt.int32
+U32 = mybir.dt.uint32
+U8 = mybir.dt.uint8
+FP8X4 = mybir.dt.float8_e4m3fn_x4
+FP4X4 = mybir.dt.float4_e2m1fn_x4
+ACT = mybir.ActivationFunctionType
+ALU = mybir.AluOpType
+
+P = 128
+PACK = 4
+ROWS = D // PACK
+QUAD = 32
+SCALE_ROWS = 4
+HALVES = M // P
+TILES = G * HALVES
+X_ROWS = slice(0, ROWS)
+DY_ROWS = slice(ROWS, P)
+VECTOR_COLUMNS = (344, 256)
+
+
+def tile_rows_browlog_kernel(
+    tc, x, w1_words, w1_scales, w2_words, w2_scales, tp, wo_words, wo_scales, dy, old, out
+):
+    nc = tc.nc
+
+    with ExitStack() as ctx:
+        sb = ctx.enter_context(tc.tile_pool(name="sb", bufs=1))
+        psum = ctx.enter_context(tc.psum_pool(name="psum", bufs=1))
+        ctx.enter_context(tc.manual_schedule())
+
+        gate_words = sb.tile([P, G * 2 * M], U8, align_bytes=64)
+        w1_tile = sb.tile([P, G * 2 * M], U8, align_bytes=64)
+        weight_scales = sb.tile([P, 2 * G * M], U8, align_bytes=64)
+        tp_rows = sb.tile([P, P], F32, align_bytes=64)
+        tp_cols = sb.tile([P, P], F32, align_bytes=64)
+        half_tp = sb.tile([P, TILES], F32)
+        minus_half_tp = sb.tile([P, TILES], F32)
+        warm = sb.tile([P, 1], F32)
+        raw = [sb.tile([P, PACK, N], F32, name="raw%d" % g) for g in range(G)]
+        grouped = [sb.tile([P, N, PACK], BF16, name="grouped%d" % g, align_bytes=64) for g in range(G)]
+        codes = [sb.tile([P, N], U32, name="codes%d" % g, align_bytes=64) for g in range(G)]
+        code_scales = [sb.tile([P, N], U8, name="code_scales%d" % g, align_bytes=64) for g in range(G)]
+        old_sb = [sb.tile([P, N], F32, name="old%d" % i) for i in range(TILES)]
+        tanh_sb = [sb.tile([P, N], F32, name="tanh%d" % i) for i in range(TILES)]
+        exp_sb = [sb.tile([P, N], F32, name="exp%d" % i) for i in range(TILES)]
+        gated = [sb.tile([P, N], F32, name="gated%d" % i) for i in range(TILES)]
+        partial = [sb.tile([P, N], F32, name="partial%d" % i) for i in range(TILES)]
+        result = [sb.tile([P, N], F32, name="result%d" % i) for i in range(TILES)]
+        exp_sum = [sb.tile([P, 1], F32, name="exp_sum%d" % i) for i in range(TILES)]
+        gated_sum = [sb.tile([P, 1], F32, name="gated_sum%d" % i) for i in range(TILES)]
+        inverse = [sb.tile([P, 1], F32, name="inverse%d" % i) for i in range(TILES)]
+        share = [sb.tile([P, 1], F32, name="share%d" % i) for i in range(TILES)]
+        x_banks = [psum.tile([P, N], F32, name="x_bank%d" % b) for b in range(6)]
+        dy_banks = [psum.tile([P, N], F32, name="dy_bank%d" % b) for b in range(2)]
+        z2_bank = [x_banks[0], x_banks[1], x_banks[4], x_banks[5]]
+        z1_bank = [x_banks[2], x_banks[3], x_banks[0], x_banks[1]]
+        c0_bank = [dy_banks[0], dy_banks[1], dy_banks[0], dy_banks[1]]
+
+        def load_words(queue, tile, rows, words):
+            queue.dma_start(
+                out=tile[rows, :].bitcast(I32).rearrange("p (g b) -> p g b", g=G),
+                in_=words.rearrange("g p b -> p g b").bitcast(I32),
+            )
+
+        def load_scales(queue, first_row, first_column, scales, quadrant):
+            row = first_row + QUAD * quadrant
+            target = weight_scales[row : row + SCALE_ROWS, first_column : first_column + G * M]
+            source = scales[:, SCALE_ROWS * quadrant : SCALE_ROWS * (quadrant + 1), :]
+            queue.dma_start(
+                out=target.bitcast(I32).rearrange("r (g m) -> r g m", g=G),
+                in_=source.rearrange("g r m -> r g m").bitcast(I32),
+            )
+
+        def load_operand(queue, g, rows, operand):
+            queue.dma_start(out=raw[g][rows], in_=operand[g].rearrange("(p j) n -> p j n", j=PACK))
+
+        def rows_of(tensor, i):
+            g, t = divmod(i, HALVES)
+            return tensor[g, t * P : (t + 1) * P, :]
+
+        def interleave(copy, g, first, last):
+            copy(
+                out=grouped[g][:, first:last, :].rearrange("p (c i) j -> p c j i", i=4),
+                in_=raw[g][:, :, first:last].rearrange("p j (c i) -> p c j i", i=4),
+            )
+
+        def quantize(g):
+            nc.vector.quantize_mx(
+                out=codes[g][:].bitcast(FP8X4),
+                scales=code_scales[g][:],
+                in_=grouped[g][:].rearrange("p n j -> p (n j)"),
+            )
+
+        def product(bank, words, rows, first_column, i):
+            g = i // HALVES
+            nc.tensor.matmul_mx(
+                out=bank[:],
+                lhsT=words[rows, 2 * P * i : 2 * P * (i + 1)].bitcast(FP4X4),
+                lhsT_scale=weight_scales[rows, first_column + P * i : first_column + P * (i + 1)],
+                rhs=codes[g][rows, :].bitcast(FP8X4),
+                rhs_scale=code_scales[g][rows, :],
+                start=True,
+                stop=True,
+            )
+
+        def products(g):
+            for i in range(g * HALVES, (g + 1) * HALVES):
+                product(z2_bank[i], gate_words, X_ROWS, 0, i)
+                product(c0_bank[i], gate_words, DY_ROWS, 0, i)
+            for i in range(g * HALVES, (g + 1) * HALVES):
+                product(z1_bank[i], w1_tile, X_ROWS, G * M, i)
+
+        def tanh_half(i):
+            nc.scalar.activation(out=tanh_sb[i][:], in_=z2_bank[i][:], func=ACT.Tanh, scale=0.5)
+
+        def exponential(i):
+            nc.scalar.activation(
+                out=exp_sb[i][:],
+                in_=z1_bank[i][:],
+                func=ACT.Exp,
+                scale=tp_cols[:, QUAD * i : QUAD * i + 1],
+                accum_out=exp_sum[i][:],
+            )
+
+        def gate(i):
+            nc.vector.scalar_tensor_tensor(
+                out=gated[i][:],
+                in0=tanh_sb[i][:],
+                scalar=1.0,
+                in1=c0_bank[i][:],
+                op0=ALU.add,
+                op1=ALU.mult,
+                accum_out=gated_sum[i][:],
+            )
+
+        def add_old(i):
+            nc.vector.scalar_tensor_tensor(
+                out=partial[i][:],
+                in0=gated[i][:],
+                scalar=half_tp[:, i : i + 1],
+                in1=old_sb[i][:],
+                op0=ALU.mult,
+                op1=ALU.add,
+            )
+
+        def invert(i):
+            nc.vector.reciprocal(out=inverse[i][:], in_=exp_sum[i][:])
+
+        def row_share(i):
+            nc.vector.tensor_scalar(
+                out=share[i][:],
+                in0=gated_sum[i][:],
+                scalar1=inverse[i][:],
+                scalar2=minus_half_tp[:, i : i + 1],
+                op0=ALU.mult,
+                op1=ALU.mult,
+            )
+
+        def finish(i):
+            nc.vector.scalar_tensor_tensor(
+                out=result[i][:],
+                in0=exp_sb[i][:],
+                scalar=share[i][:],
+                in1=partial[i][:],
+                op0=ALU.mult,
+                op1=ALU.add,
+            )
+            nc.sync.dma_start(out=rows_of(out, i), in_=result[i][:])
+
+        nc.vector.memset(weight_scales[:].bitcast(I32), 0)
+        nc.gpsimd.memset(tp_rows[:], 0.0)
+        load_words(nc.sync, gate_words, X_ROWS, w2_words)
+        load_words(nc.scalar, gate_words, DY_ROWS, wo_words)
+        load_operand(nc.sync, 0, X_ROWS, x)
+        load_operand(nc.scalar, 0, DY_ROWS, dy)
+        for quadrant in range(ROWS // QUAD):
+            load_scales(nc.sync, 0, 0, w2_scales, quadrant)
+            load_scales(nc.scalar, ROWS, 0, wo_scales, quadrant)
+        nc.gpsimd.dma_start(
+            out=tp_rows[0:P:QUAD, :].rearrange("q (c i) -> q c i", i=QUAD),
+            in_=tp.rearrange("g (t q i) o -> q (g t) (i o)", t=HALVES, i=QUAD),
+        )
+        load_words(nc.gpsimd, w1_tile, X_ROWS, w1_words)
+        nc.vector.memset(warm[:], 0.0)
+        nc.scalar.activation(out=warm[:], in_=warm[:], func=ACT.Exp)
+        load_operand(nc.sync, 1, X_ROWS, x)
+        load_operand(nc.scalar, 1, DY_ROWS, dy)
+        for quadrant in range(ROWS // QUAD):
+            load_scales(nc.sync, 0, G * M, w1_scales, quadrant)
+        for i in range(TILES):
+            nc.sync.dma_start(out=old_sb[i][:], in_=rows_of(old, i))
+
+        interleave(nc.vector.tensor_copy, 0, 0, VECTOR_COLUMNS[0])
+        interleave(nc.scalar.copy, 0, VECTOR_COLUMNS[0], N)
+        quantize(0)
+        products(0)
+        nc.vector.transpose(out=tp_cols[:], in_=tp_rows[:])
+        nc.vector.tensor_scalar(
+            out=half_tp[:], in0=tp_cols[:, 0:P:QUAD], scalar1=0.5, scalar2=None, op0=ALU.mult
+        )
+        nc.vector.tensor_scalar(
+            out=minus_half_tp[:], in0=tp_cols[:, 0:P:QUAD], scalar1=-0.5, scalar2=None, op0=ALU.mult
+        )
+        interleave(nc.vector.tensor_copy, 1, 0, VECTOR_COLUMNS[1])
+        tanh_half(0)
+        tanh_half(1)
+        exponential(0)
+        interleave(nc.scalar.copy, 1, VECTOR_COLUMNS[1], N)
+        exponential(1)
+        gate(0)
+        gate(1)
+        invert(0)
+        add_old(0)
+        row_share(0)
+        add_old(1)
+        quantize(1)
+        products(1)
+        invert(1)
+        finish(0)
+        row_share(1)
+        tanh_half(2)
+        tanh_half(3)
+        exponential(2)
+        exponential(3)
+        gate(2)
+        finish(1)
+        gate(3)
+        invert(2)
+        add_old(2)
+        row_share(2)
+        invert(3)
+        add_old(3)
+        row_share(3)
+        finish(2)
+        finish(3)

@@ -22,9 +22,10 @@ QUAD = 32
 SCALE_ROWS = 4
 HALVES = M // P
 TILES = G * HALVES
-X_ROWS = slice(0, ROWS)
-DY_ROWS = slice(ROWS, P)
-VECTOR_COLUMNS = (344, 256)
+ORDER = [g * HALVES + t for t in range(HALVES) for g in range(G)]
+VECTOR_PIECE = (0, 256)
+SCALAR_PIECES = ((256, 384), (384, 512))
+PIECES = (SCALAR_PIECES[0], VECTOR_PIECE, SCALAR_PIECES[1])
 
 
 def tile_rows_browlog_kernel(
@@ -37,87 +38,93 @@ def tile_rows_browlog_kernel(
         psum = ctx.enter_context(tc.psum_pool(name="psum", bufs=1))
         ctx.enter_context(tc.manual_schedule())
 
-        gate_words = sb.tile([P, G * 2 * M], U8, align_bytes=64)
-        w1_tile = sb.tile([P, G * 2 * M], U8, align_bytes=64)
-        weight_scales = sb.tile([P, 2 * G * M], U8, align_bytes=64)
+        words = {w: sb.tile([P, 2 * M], U8, name=w + "_words", align_bytes=64) for w in ("w1", "w2", "wo")}
+        all_scales = sb.tile([P, 3 * M], U8, align_bytes=64)
+        scale_column = {"w1": 0, "w2": M, "wo": 2 * M}
         tp_rows = sb.tile([P, P], F32, align_bytes=64)
         tp_cols = sb.tile([P, P], F32, align_bytes=64)
         half_tp = sb.tile([P, TILES], F32)
         minus_half_tp = sb.tile([P, TILES], F32)
         warm = sb.tile([P, 1], F32)
-        raw = [sb.tile([P, PACK, N], F32, name="raw%d" % g) for g in range(G)]
-        grouped = [sb.tile([P, N, PACK], BF16, name="grouped%d" % g, align_bytes=64) for g in range(G)]
-        codes = [sb.tile([P, N], U32, name="codes%d" % g, align_bytes=64) for g in range(G)]
-        code_scales = [sb.tile([P, N], U8, name="code_scales%d" % g, align_bytes=64) for g in range(G)]
+        raw = {a: sb.tile([P, PACK, N], F32, name=a + "_raw") for a in ("x", "dy")}
+        grouped = {
+            (a, first): sb.tile([P, last - first, PACK], BF16, name="%s_grouped%d" % (a, first), align_bytes=64)
+            for a in ("x", "dy")
+            for first, last in PIECES
+        }
+        codes = {a: sb.tile([P, N], U32, name=a + "_codes", align_bytes=64) for a in ("x", "dy")}
+        code_scales = {a: sb.tile([P, N], U8, name=a + "_code_scales", align_bytes=64) for a in ("x", "dy")}
         old_sb = [sb.tile([P, N], F32, name="old%d" % i) for i in range(TILES)]
         tanh_sb = [sb.tile([P, N], F32, name="tanh%d" % i) for i in range(TILES)]
         exp_sb = [sb.tile([P, N], F32, name="exp%d" % i) for i in range(TILES)]
         gated = [sb.tile([P, N], F32, name="gated%d" % i) for i in range(TILES)]
         partial = [sb.tile([P, N], F32, name="partial%d" % i) for i in range(TILES)]
         result = [sb.tile([P, N], F32, name="result%d" % i) for i in range(TILES)]
-        exp_sum = [sb.tile([P, 1], F32, name="exp_sum%d" % i) for i in range(TILES)]
-        gated_sum = [sb.tile([P, 1], F32, name="gated_sum%d" % i) for i in range(TILES)]
-        inverse = [sb.tile([P, 1], F32, name="inverse%d" % i) for i in range(TILES)]
-        share = [sb.tile([P, 1], F32, name="share%d" % i) for i in range(TILES)]
-        x_banks = [psum.tile([P, N], F32, name="x_bank%d" % b) for b in range(6)]
-        dy_banks = [psum.tile([P, N], F32, name="dy_bank%d" % b) for b in range(2)]
-        z2_bank = [x_banks[0], x_banks[1], x_banks[4], x_banks[5]]
-        z1_bank = [x_banks[2], x_banks[3], x_banks[0], x_banks[1]]
-        c0_bank = [dy_banks[0], dy_banks[1], dy_banks[0], dy_banks[1]]
+        scaled_gate = sb.tile([P, N], F32)
+        exp_sums = [sb.tile([P, G], F32, name="exp_sums%d" % t) for t in range(HALVES)]
+        gated_sums = [sb.tile([P, G], F32, name="gated_sums%d" % t) for t in range(HALVES)]
+        inverses = [sb.tile([P, G], F32, name="inverses%d" % t) for t in range(HALVES)]
+        numerators = [sb.tile([P, G], F32, name="numerators%d" % t) for t in range(HALVES)]
+        shares = [sb.tile([P, G], F32, name="shares%d" % t) for t in range(HALVES)]
+        banks = [[psum.tile([P, N], F32, name="bank%d_%d" % (g, b)) for b in range(4)] for g in range(G)]
+        z2_bank = [banks[i // HALVES][(0, 1)[i % HALVES]] for i in range(TILES)]
+        z1_bank = [banks[i // HALVES][(3, 1)[i % HALVES]] for i in range(TILES)]
+        c0_bank = [banks[i // HALVES][(2, 0)[i % HALVES]] for i in range(TILES)]
 
-        def load_words(queue, tile, rows, words):
+        def load_words(queue, w, source):
             queue.dma_start(
-                out=tile[rows, :].bitcast(I32).rearrange("p (g b) -> p g b", g=G),
-                in_=words.rearrange("g p b -> p g b").bitcast(I32),
+                out=words[w][:].bitcast(I32), in_=source.rearrange("g p b -> (g p) b").bitcast(I32)
             )
 
-        def load_scales(queue, first_row, first_column, scales, quadrant):
-            row = first_row + QUAD * quadrant
-            target = weight_scales[row : row + SCALE_ROWS, first_column : first_column + G * M]
-            source = scales[:, SCALE_ROWS * quadrant : SCALE_ROWS * (quadrant + 1), :]
-            queue.dma_start(
-                out=target.bitcast(I32).rearrange("r (g m) -> r g m", g=G),
-                in_=source.rearrange("g r m -> r g m").bitcast(I32),
-            )
+        def load_scales(queue, w, source, quadrants):
+            rows = source.rearrange("g f m -> (g f) m")
+            for q in quadrants:
+                queue.dma_start(
+                    out=all_scales[QUAD * q : QUAD * q + SCALE_ROWS, scale_column[w] : scale_column[w] + M].bitcast(I32),
+                    in_=rows[SCALE_ROWS * q : SCALE_ROWS * (q + 1), :].bitcast(I32),
+                )
 
-        def load_operand(queue, g, rows, operand):
-            queue.dma_start(out=raw[g][rows], in_=operand[g].rearrange("(p j) n -> p j n", j=PACK))
+        def load_operand(a, source):
+            nc.sync.dma_start(out=raw[a][:], in_=source.rearrange("g (p j) n -> (g p) j n", j=PACK))
+
+        def column(tiles, i):
+            g, t = divmod(i, HALVES)
+            return tiles[t][:, g : g + 1]
 
         def rows_of(tensor, i):
             g, t = divmod(i, HALVES)
             return tensor[g, t * P : (t + 1) * P, :]
 
-        def interleave(copy, g, first, last):
+        def interleave(copy, a, first, last):
             copy(
-                out=grouped[g][:, first:last, :].rearrange("p (c i) j -> p c j i", i=4),
-                in_=raw[g][:, :, first:last].rearrange("p j (c i) -> p c j i", i=4),
+                out=grouped[a, first][:].rearrange("p (c i) j -> p c j i", i=4),
+                in_=raw[a][:, :, first:last].rearrange("p j (c i) -> p c j i", i=4),
             )
 
-        def quantize(g):
-            nc.vector.quantize_mx(
-                out=codes[g][:].bitcast(FP8X4),
-                scales=code_scales[g][:],
-                in_=grouped[g][:].rearrange("p n j -> p (n j)"),
-            )
+        def quantize(a):
+            interleave(nc.vector.tensor_copy, a, *VECTOR_PIECE)
+            for piece in SCALAR_PIECES:
+                interleave(nc.scalar.copy, a, *piece)
+            for first, last in PIECES:
+                nc.vector.quantize_mx(
+                    out=codes[a][:, first:last].bitcast(FP8X4),
+                    scales=code_scales[a][:, first:last],
+                    in_=grouped[a, first][:].rearrange("p n j -> p (n j)"),
+                )
 
-        def product(bank, words, rows, first_column, i):
-            g = i // HALVES
+        def product(bank, w, a, i):
+            g, t = divmod(i, HALVES)
+            rows = slice(g * ROWS, (g + 1) * ROWS)
+            column = scale_column[w] + P * t
             nc.tensor.matmul_mx(
-                out=bank[:],
-                lhsT=words[rows, 2 * P * i : 2 * P * (i + 1)].bitcast(FP4X4),
-                lhsT_scale=weight_scales[rows, first_column + P * i : first_column + P * (i + 1)],
-                rhs=codes[g][rows, :].bitcast(FP8X4),
-                rhs_scale=code_scales[g][rows, :],
+                out=bank[i][:],
+                lhsT=words[w][rows, 2 * P * t : 2 * P * (t + 1)].bitcast(FP4X4),
+                lhsT_scale=all_scales[rows, column : column + P],
+                rhs=codes[a][rows, :].bitcast(FP8X4),
+                rhs_scale=code_scales[a][rows, :],
                 start=True,
                 stop=True,
             )
-
-        def products(g):
-            for i in range(g * HALVES, (g + 1) * HALVES):
-                product(z2_bank[i], gate_words, X_ROWS, 0, i)
-                product(c0_bank[i], gate_words, DY_ROWS, 0, i)
-            for i in range(g * HALVES, (g + 1) * HALVES):
-                product(z1_bank[i], w1_tile, X_ROWS, G * M, i)
 
         def tanh_half(i):
             nc.scalar.activation(out=tanh_sb[i][:], in_=z2_bank[i][:], func=ACT.Tanh, scale=0.5)
@@ -128,7 +135,18 @@ def tile_rows_browlog_kernel(
                 in_=z1_bank[i][:],
                 func=ACT.Exp,
                 scale=tp_cols[:, QUAD * i : QUAD * i + 1],
-                accum_out=exp_sum[i][:],
+                accum_out=column(exp_sums, i),
+            )
+
+        def gate_scaled(i):
+            nc.vector.scalar_tensor_tensor(
+                out=gated[i][:],
+                in0=c0_bank[i][:],
+                scalar=1.0,
+                in1=scaled_gate[:],
+                op0=ALU.mult,
+                op1=ALU.mult,
+                accum_out=column(gated_sums, i),
             )
 
         def gate(i):
@@ -139,7 +157,7 @@ def tile_rows_browlog_kernel(
                 in1=c0_bank[i][:],
                 op0=ALU.add,
                 op1=ALU.mult,
-                accum_out=gated_sum[i][:],
+                accum_out=column(gated_sums, i),
             )
 
         def add_old(i):
@@ -152,57 +170,54 @@ def tile_rows_browlog_kernel(
                 op1=ALU.add,
             )
 
-        def invert(i):
-            nc.vector.reciprocal(out=inverse[i][:], in_=exp_sum[i][:])
-
-        def row_share(i):
-            nc.vector.tensor_scalar(
-                out=share[i][:],
-                in0=gated_sum[i][:],
-                scalar1=inverse[i][:],
-                scalar2=minus_half_tp[:, i : i + 1],
-                op0=ALU.mult,
-                op1=ALU.mult,
-            )
-
         def finish(i):
             nc.vector.scalar_tensor_tensor(
                 out=result[i][:],
                 in0=exp_sb[i][:],
-                scalar=share[i][:],
+                scalar=column(shares, i),
                 in1=partial[i][:],
                 op0=ALU.mult,
                 op1=ALU.add,
             )
             nc.sync.dma_start(out=rows_of(out, i), in_=result[i][:])
 
-        nc.vector.memset(weight_scales[:].bitcast(I32), 0)
+        def invert(t):
+            nc.vector.reciprocal(out=inverses[t][:], in_=exp_sums[t][:])
+
+        def row_shares(pair):
+            for i in pair:
+                factor = -1.0 if i == ORDER[0] else minus_half_tp[:, i : i + 1]
+                multiply(column(numerators, i), column(gated_sums, i), factor)
+            for i in pair:
+                multiply(column(shares, i), column(numerators, i), column(inverses, i))
+
+        def multiply(target, source, factor):
+            nc.scalar.activation(out=target, in_=source, func=ACT.Copy, scale=factor)
+
+        nc.vector.memset(all_scales[:].bitcast(I32), 0)
         nc.gpsimd.memset(tp_rows[:], 0.0)
-        load_words(nc.sync, gate_words, X_ROWS, w2_words)
-        load_words(nc.scalar, gate_words, DY_ROWS, wo_words)
-        load_operand(nc.sync, 0, X_ROWS, x)
-        load_operand(nc.scalar, 0, DY_ROWS, dy)
-        for quadrant in range(ROWS // QUAD):
-            load_scales(nc.sync, 0, 0, w2_scales, quadrant)
-            load_scales(nc.scalar, ROWS, 0, wo_scales, quadrant)
         nc.gpsimd.dma_start(
             out=tp_rows[0:P:QUAD, :].rearrange("q (c i) -> q c i", i=QUAD),
             in_=tp.rearrange("g (t q i) o -> q (g t) (i o)", t=HALVES, i=QUAD),
         )
-        load_words(nc.gpsimd, w1_tile, X_ROWS, w1_words)
+        load_scales(nc.gpsimd, "wo", wo_scales, (2, 3))
+        load_operand("x", x)
+        load_words(nc.scalar, "w2", w2_words)
+        load_scales(nc.scalar, "w2", w2_scales, range(4))
+        load_operand("dy", dy)
+        load_words(nc.sync, "wo", wo_words)
+        load_scales(nc.sync, "wo", wo_scales, (0, 1))
+        load_words(nc.sync, "w1", w1_words)
+        load_scales(nc.sync, "w1", w1_scales, range(4))
+        for i in ORDER:
+            nc.sync.dma_start(out=old_sb[i][:], in_=rows_of(old, i))
         nc.vector.memset(warm[:], 0.0)
         nc.scalar.activation(out=warm[:], in_=warm[:], func=ACT.Exp)
-        load_operand(nc.sync, 1, X_ROWS, x)
-        load_operand(nc.scalar, 1, DY_ROWS, dy)
-        for quadrant in range(ROWS // QUAD):
-            load_scales(nc.sync, 0, G * M, w1_scales, quadrant)
-        for i in range(TILES):
-            nc.sync.dma_start(out=old_sb[i][:], in_=rows_of(old, i))
 
-        interleave(nc.vector.tensor_copy, 0, 0, VECTOR_COLUMNS[0])
-        interleave(nc.scalar.copy, 0, VECTOR_COLUMNS[0], N)
-        quantize(0)
-        products(0)
+        a, b, c, d = ORDER
+        quantize("x")
+        for i in ORDER:
+            product(z2_bank, "w2", "x", i)
         nc.vector.transpose(out=tp_cols[:], in_=tp_rows[:])
         nc.vector.tensor_scalar(
             out=half_tp[:], in0=tp_cols[:, 0:P:QUAD], scalar1=0.5, scalar2=None, op0=ALU.mult
@@ -210,35 +225,40 @@ def tile_rows_browlog_kernel(
         nc.vector.tensor_scalar(
             out=minus_half_tp[:], in0=tp_cols[:, 0:P:QUAD], scalar1=-0.5, scalar2=None, op0=ALU.mult
         )
-        interleave(nc.vector.tensor_copy, 1, 0, VECTOR_COLUMNS[1])
-        tanh_half(0)
-        tanh_half(1)
-        exponential(0)
-        interleave(nc.scalar.copy, 1, VECTOR_COLUMNS[1], N)
-        exponential(1)
-        gate(0)
-        gate(1)
+        quantize("dy")
+        product(c0_bank, "wo", "dy", a)
+        product(c0_bank, "wo", "dy", b)
+        for i in ORDER:
+            tanh_half(i)
+        product(c0_bank, "wo", "dy", c)
+        product(c0_bank, "wo", "dy", d)
+        for i in ORDER:
+            product(z1_bank, "w1", "x", i)
+        nc.vector.tensor_scalar(
+            out=scaled_gate[:],
+            in0=tanh_sb[a][:],
+            scalar1=half_tp[:, a : a + 1],
+            scalar2=half_tp[:, a : a + 1],
+            op0=ALU.mult,
+            op1=ALU.add,
+        )
+        exponential(a)
+        exponential(b)
+        gate_scaled(a)
+        nc.gpsimd.tensor_tensor(out=partial[a][:], in0=gated[a][:], in1=old_sb[a][:], op=ALU.add)
+        gate(b)
+        gate(c)
+        gate(d)
+        add_old(b)
+        add_old(c)
         invert(0)
-        add_old(0)
-        row_share(0)
-        add_old(1)
-        quantize(1)
-        products(1)
+        row_shares((a, b))
+        exponential(c)
+        exponential(d)
+        add_old(d)
+        finish(a)
         invert(1)
-        finish(0)
-        row_share(1)
-        tanh_half(2)
-        tanh_half(3)
-        exponential(2)
-        exponential(3)
-        gate(2)
-        finish(1)
-        gate(3)
-        invert(2)
-        add_old(2)
-        row_share(2)
-        invert(3)
-        add_old(3)
-        row_share(3)
-        finish(2)
-        finish(3)
+        row_shares((c, d))
+        finish(b)
+        finish(c)
+        finish(d)

@@ -23,9 +23,9 @@ SCALE_ROWS = 4
 HALVES = M // P
 TILES = G * HALVES
 ORDER = [g * HALVES + t for t in range(HALVES) for g in range(G)]
-VECTOR_PIECE = (0, 256)
-SCALAR_PIECES = ((256, 384), (384, 512))
-PIECES = (SCALAR_PIECES[0], VECTOR_PIECE, SCALAR_PIECES[1])
+PIECES = ((0, 128), (128, 384), (384, 512))
+VECTOR_COPIES = ((1, 128, 384), (2, 384, 448))
+SCALAR_COPIES = ((0, 0, 128), (2, 448, 512))
 
 
 def tile_rows_browlog_kernel(
@@ -61,25 +61,25 @@ def tile_rows_browlog_kernel(
         partial = [sb.tile([P, N], F32, name="partial%d" % i) for i in range(TILES)]
         result = [sb.tile([P, N], F32, name="result%d" % i) for i in range(TILES)]
         scaled_gate = sb.tile([P, N], F32)
-        exp_sums = [sb.tile([P, G], F32, name="exp_sums%d" % t) for t in range(HALVES)]
-        gated_sums = [sb.tile([P, G], F32, name="gated_sums%d" % t) for t in range(HALVES)]
-        inverses = [sb.tile([P, G], F32, name="inverses%d" % t) for t in range(HALVES)]
-        numerators = [sb.tile([P, G], F32, name="numerators%d" % t) for t in range(HALVES)]
-        shares = [sb.tile([P, G], F32, name="shares%d" % t) for t in range(HALVES)]
+        exp_sums = [sb.tile([P, 1], F32, name="exp_sums%d" % i) for i in range(TILES)]
+        gated_sums = [sb.tile([P, 1], F32, name="gated_sums%d" % i) for i in range(TILES)]
+        inverses = [sb.tile([P, 1], F32, name="inverses%d" % i) for i in range(TILES)]
+        numerators = [sb.tile([P, 1], F32, name="numerators%d" % i) for i in range(TILES)]
+        shares = [sb.tile([P, 1], F32, name="shares%d" % i) for i in range(TILES)]
         banks = [[psum.tile([P, N], F32, name="bank%d_%d" % (g, b)) for b in range(4)] for g in range(G)]
         z2_bank = [banks[i // HALVES][(0, 1)[i % HALVES]] for i in range(TILES)]
         z1_bank = [banks[i // HALVES][(3, 1)[i % HALVES]] for i in range(TILES)]
         c0_bank = [banks[i // HALVES][(2, 0)[i % HALVES]] for i in range(TILES)]
 
-        def load_words(queue, w, source):
-            queue.dma_start(
+        def load_words(w, source):
+            nc.sync.dma_start(
                 out=words[w][:].bitcast(I32), in_=source.rearrange("g p b -> (g p) b").bitcast(I32)
             )
 
-        def load_scales(queue, w, source, quadrants):
+        def load_scales(w, source, quadrants):
             rows = source.rearrange("g f m -> (g f) m")
             for q in quadrants:
-                queue.dma_start(
+                nc.sync.dma_start(
                     out=all_scales[QUAD * q : QUAD * q + SCALE_ROWS, scale_column[w] : scale_column[w] + M].bitcast(I32),
                     in_=rows[SCALE_ROWS * q : SCALE_ROWS * (q + 1), :].bitcast(I32),
                 )
@@ -87,30 +87,32 @@ def tile_rows_browlog_kernel(
         def load_operand(a, source):
             nc.sync.dma_start(out=raw[a][:], in_=source.rearrange("g (p j) n -> (g p) j n", j=PACK))
 
-        def column(tiles, i):
-            g, t = divmod(i, HALVES)
-            return tiles[t][:, g : g + 1]
-
         def rows_of(tensor, i):
             g, t = divmod(i, HALVES)
             return tensor[g, t * P : (t + 1) * P, :]
 
-        def interleave(copy, a, first, last):
+        def load_old(i):
+            nc.sync.dma_start(out=old_sb[i][:], in_=rows_of(old, i))
+
+        def interleave(copy, a, piece, first, last):
+            start = PIECES[piece][0]
             copy(
-                out=grouped[a, first][:].rearrange("p (c i) j -> p c j i", i=4),
+                out=grouped[a, start][:, first - start : last - start, :].rearrange("p (c i) j -> p c j i", i=4),
                 in_=raw[a][:, :, first:last].rearrange("p j (c i) -> p c j i", i=4),
             )
 
-        def quantize(a):
-            interleave(nc.vector.tensor_copy, a, *VECTOR_PIECE)
-            for piece in SCALAR_PIECES:
-                interleave(nc.scalar.copy, a, *piece)
-            for first, last in PIECES:
-                nc.vector.quantize_mx(
-                    out=codes[a][:, first:last].bitcast(FP8X4),
-                    scales=code_scales[a][:, first:last],
-                    in_=grouped[a, first][:].rearrange("p n j -> p (n j)"),
-                )
+        def interleave_all(a):
+            for columns in VECTOR_COPIES:
+                interleave(nc.vector.tensor_copy, a, *columns)
+            for columns in SCALAR_COPIES:
+                interleave(nc.scalar.copy, a, *columns)
+
+        def quantize(a, first, last):
+            nc.vector.quantize_mx(
+                out=codes[a][:, first:last].bitcast(FP8X4),
+                scales=code_scales[a][:, first:last],
+                in_=grouped[a, first][:].rearrange("p n j -> p (n j)"),
+            )
 
         def product(bank, w, a, i):
             g, t = divmod(i, HALVES)
@@ -135,7 +137,7 @@ def tile_rows_browlog_kernel(
                 in_=z1_bank[i][:],
                 func=ACT.Exp,
                 scale=tp_cols[:, QUAD * i : QUAD * i + 1],
-                accum_out=column(exp_sums, i),
+                accum_out=exp_sums[i][:],
             )
 
         def gate_scaled(i):
@@ -146,7 +148,7 @@ def tile_rows_browlog_kernel(
                 in1=scaled_gate[:],
                 op0=ALU.mult,
                 op1=ALU.mult,
-                accum_out=column(gated_sums, i),
+                accum_out=gated_sums[i][:],
             )
 
         def gate(i):
@@ -157,7 +159,7 @@ def tile_rows_browlog_kernel(
                 in1=c0_bank[i][:],
                 op0=ALU.add,
                 op1=ALU.mult,
-                accum_out=column(gated_sums, i),
+                accum_out=gated_sums[i][:],
             )
 
         def add_old(i):
@@ -174,22 +176,22 @@ def tile_rows_browlog_kernel(
             nc.vector.scalar_tensor_tensor(
                 out=result[i][:],
                 in0=exp_sb[i][:],
-                scalar=column(shares, i),
+                scalar=shares[i][:],
                 in1=partial[i][:],
                 op0=ALU.mult,
                 op1=ALU.add,
             )
             nc.sync.dma_start(out=rows_of(out, i), in_=result[i][:])
 
-        def invert(t):
-            nc.vector.reciprocal(out=inverses[t][:], in_=exp_sums[t][:])
+        def invert(i):
+            nc.vector.reciprocal(out=inverses[i][:], in_=exp_sums[i][:])
 
-        def row_shares(pair):
-            for i in pair:
-                factor = -1.0 if i == ORDER[0] else minus_half_tp[:, i : i + 1]
-                multiply(column(numerators, i), column(gated_sums, i), factor)
-            for i in pair:
-                multiply(column(shares, i), column(numerators, i), column(inverses, i))
+        def numerator(i):
+            factor = -1.0 if i == ORDER[0] else minus_half_tp[:, i : i + 1]
+            multiply(numerators[i][:], gated_sums[i][:], factor)
+
+        def share(i):
+            multiply(shares[i][:], numerators[i][:], inverses[i][:])
 
         def multiply(target, source, factor):
             nc.scalar.activation(out=target, in_=source, func=ACT.Copy, scale=factor)
@@ -200,32 +202,35 @@ def tile_rows_browlog_kernel(
             out=tp_rows[0:P:QUAD, :].rearrange("q (c i) -> q c i", i=QUAD),
             in_=tp.rearrange("g (t q i) o -> q (g t) (i o)", t=HALVES, i=QUAD),
         )
-        load_scales(nc.gpsimd, "wo", wo_scales, (2, 3))
+        a, b, c, d = ORDER
         load_operand("x", x)
-        load_words(nc.scalar, "w2", w2_words)
-        load_scales(nc.scalar, "w2", w2_scales, range(4))
+        load_words("w2", w2_words)
+        load_scales("w2", w2_scales, range(4))
         load_operand("dy", dy)
-        load_words(nc.sync, "wo", wo_words)
-        load_scales(nc.sync, "wo", wo_scales, (0, 1))
-        load_words(nc.sync, "w1", w1_words)
-        load_scales(nc.sync, "w1", w1_scales, range(4))
-        for i in ORDER:
-            nc.sync.dma_start(out=old_sb[i][:], in_=rows_of(old, i))
+        load_words("wo", wo_words)
+        load_scales("wo", wo_scales, range(4))
+        load_words("w1", w1_words)
+        load_scales("w1", w1_scales, range(1))
+        load_old(a)
+        load_scales("w1", w1_scales, range(1, 4))
+        for i in (b, c, d):
+            load_old(i)
         nc.vector.memset(warm[:], 0.0)
         nc.scalar.activation(out=warm[:], in_=warm[:], func=ACT.Exp)
 
-        a, b, c, d = ORDER
-        quantize("x")
+        interleave_all("x")
+        for piece in PIECES:
+            quantize("x", *piece)
         for i in ORDER:
             product(z2_bank, "w2", "x", i)
+        interleave_all("dy")
+        for piece in PIECES[:-1]:
+            quantize("dy", *piece)
         nc.vector.transpose(out=tp_cols[:], in_=tp_rows[:])
+        quantize("dy", *PIECES[-1])
         nc.vector.tensor_scalar(
             out=half_tp[:], in0=tp_cols[:, 0:P:QUAD], scalar1=0.5, scalar2=None, op0=ALU.mult
         )
-        nc.vector.tensor_scalar(
-            out=minus_half_tp[:], in0=tp_cols[:, 0:P:QUAD], scalar1=-0.5, scalar2=None, op0=ALU.mult
-        )
-        quantize("dy")
         product(c0_bank, "wo", "dy", a)
         product(c0_bank, "wo", "dy", b)
         for i in ORDER:
@@ -242,23 +247,30 @@ def tile_rows_browlog_kernel(
             op0=ALU.mult,
             op1=ALU.add,
         )
-        exponential(a)
-        exponential(b)
+        multiply(minus_half_tp[:], tp_cols[:, 0:P:QUAD], -0.5)
         gate_scaled(a)
         nc.gpsimd.tensor_tensor(out=partial[a][:], in0=gated[a][:], in1=old_sb[a][:], op=ALU.add)
-        gate(b)
-        gate(c)
-        gate(d)
+        for i in (b, c, d):
+            gate(i)
+        for i in (a, b, c):
+            numerator(i)
+        exponential(a)
+        numerator(d)
+        exponential(b)
         add_old(b)
-        add_old(c)
-        invert(0)
-        row_shares((a, b))
+        invert(a)
+        share(a)
         exponential(c)
+        add_old(c)
+        invert(b)
+        share(b)
         exponential(d)
         add_old(d)
         finish(a)
-        invert(1)
-        row_shares((c, d))
+        invert(c)
+        share(c)
         finish(b)
+        invert(d)
+        share(d)
         finish(c)
         finish(d)

@@ -61,9 +61,9 @@ def tile_rows_browlog_kernel(
         partial = [sb.tile([P, N], F32, name="partial%d" % i) for i in range(TILES)]
         result = [sb.tile([P, N], F32, name="result%d" % i) for i in range(TILES)]
         scaled_gate = sb.tile([P, N], F32)
-        exp_sums = [sb.tile([P, 1], F32, name="exp_sums%d" % i) for i in range(TILES)]
-        gated_sums = [sb.tile([P, 1], F32, name="gated_sums%d" % i) for i in range(TILES)]
-        inverses = [sb.tile([P, 1], F32, name="inverses%d" % i) for i in range(TILES)]
+        exp_sums = sb.tile([P, TILES], F32)
+        gated_sums = {i: sb.tile([P, 1], F32, name="gated_sums%d" % i) for i in ORDER[:2]}
+        inverses = sb.tile([P, TILES], F32)
         numerators = [sb.tile([P, 1], F32, name="numerators%d" % i) for i in range(TILES)]
         shares = [sb.tile([P, 1], F32, name="shares%d" % i) for i in range(TILES)]
         banks = [[psum.tile([P, N], F32, name="bank%d_%d" % (g, b)) for b in range(4)] for g in range(G)]
@@ -137,7 +137,7 @@ def tile_rows_browlog_kernel(
                 in_=z1_bank[i][:],
                 func=ACT.Exp,
                 scale=tp_cols[:, QUAD * i : QUAD * i + 1],
-                accum_out=exp_sums[i][:],
+                accum_out=exp_sums[:, i : i + 1],
             )
 
         def gate_scaled(i):
@@ -151,7 +151,7 @@ def tile_rows_browlog_kernel(
                 accum_out=gated_sums[i][:],
             )
 
-        def gate(i):
+        def gate(i, row_sum):
             nc.vector.scalar_tensor_tensor(
                 out=gated[i][:],
                 in0=tanh_sb[i][:],
@@ -159,7 +159,7 @@ def tile_rows_browlog_kernel(
                 in1=c0_bank[i][:],
                 op0=ALU.add,
                 op1=ALU.mult,
-                accum_out=gated_sums[i][:],
+                accum_out=row_sum,
             )
 
         def add_old(i):
@@ -183,15 +183,21 @@ def tile_rows_browlog_kernel(
             )
             nc.sync.dma_start(out=rows_of(out, i), in_=result[i][:])
 
-        def invert(i):
-            nc.vector.reciprocal(out=inverses[i][:], in_=exp_sums[i][:])
-
         def numerator(i):
             factor = -1.0 if i == ORDER[0] else minus_half_tp[:, i : i + 1]
             multiply(numerators[i][:], gated_sums[i][:], factor)
 
+        def summed_numerator(i):
+            nc.scalar.activation(
+                out=tanh_sb[i][:],
+                in_=gated[i][:],
+                func=ACT.Copy,
+                scale=minus_half_tp[:, i : i + 1],
+                accum_out=numerators[i][:],
+            )
+
         def share(i):
-            multiply(shares[i][:], numerators[i][:], inverses[i][:])
+            multiply(shares[i][:], numerators[i][:], inverses[:, i : i + 1])
 
         def multiply(target, source, factor):
             nc.scalar.activation(out=target, in_=source, func=ACT.Copy, scale=factor)
@@ -223,14 +229,13 @@ def tile_rows_browlog_kernel(
             quantize("x", *piece)
         for i in ORDER:
             product(z2_bank, "w2", "x", i)
-        interleave_all("dy")
-        for piece in PIECES[:-1]:
-            quantize("dy", *piece)
         nc.vector.transpose(out=tp_cols[:], in_=tp_rows[:])
-        quantize("dy", *PIECES[-1])
         nc.vector.tensor_scalar(
             out=half_tp[:], in0=tp_cols[:, 0:P:QUAD], scalar1=0.5, scalar2=None, op0=ALU.mult
         )
+        interleave_all("dy")
+        for piece in PIECES:
+            quantize("dy", *piece)
         product(c0_bank, "wo", "dy", a)
         product(c0_bank, "wo", "dy", b)
         for i in ORDER:
@@ -248,29 +253,24 @@ def tile_rows_browlog_kernel(
             op1=ALU.add,
         )
         multiply(minus_half_tp[:], tp_cols[:, 0:P:QUAD], -0.5)
+        for i in ORDER:
+            exponential(i)
         gate_scaled(a)
         nc.gpsimd.tensor_tensor(out=partial[a][:], in0=gated[a][:], in1=old_sb[a][:], op=ALU.add)
-        for i in (b, c, d):
-            gate(i)
-        for i in (a, b, c):
-            numerator(i)
-        exponential(a)
-        numerator(d)
-        exponential(b)
+        gate(b, gated_sums[b][:])
+        gate(c, None)
+        gate(d, None)
         add_old(b)
-        invert(a)
-        share(a)
-        exponential(c)
         add_old(c)
-        invert(b)
-        share(b)
-        exponential(d)
+        nc.vector.reciprocal(out=inverses[:], in_=exp_sums[:])
         add_old(d)
-        finish(a)
-        invert(c)
+        numerator(a)
+        numerator(b)
+        summed_numerator(c)
+        share(a)
+        share(b)
+        summed_numerator(d)
         share(c)
-        finish(b)
-        invert(d)
         share(d)
-        finish(c)
-        finish(d)
+        for i in ORDER:
+            finish(i)

from contextlib import ExitStack

import concourse.mybir as mybir

G, D, M, N = 2, 256, 256, 512
FLOPS = 3 * 2 * G * D * M * N

F32 = mybir.dt.float32
BF16 = mybir.dt.bfloat16
I32 = mybir.dt.int32
U32 = mybir.dt.uint32
U8 = mybir.dt.uint8
FP8X4 = mybir.dt.float8_e4m3fn_x4
FP4X4 = mybir.dt.float4_e2m1fn_x4
ACT = mybir.ActivationFunctionType
ALU = mybir.AluOpType

P = 128
PACK = 4
ROWS = D // PACK
QUAD = 32
SCALE_ROWS = 4
HALVES = M // P
TILES = G * HALVES
ORDER = [g * HALVES + t for t in range(HALVES) for g in range(G)]
PIECES = ((0, 128), (128, 384), (384, 512))
VECTOR_COPIES = ((1, 128, 384), (2, 384, 448))
SCALAR_COPIES = ((0, 0, 128), (2, 448, 512))


def tile_rows_browlog_kernel(
    tc, x, w1_words, w1_scales, w2_words, w2_scales, tp, wo_words, wo_scales, dy, old, out
):
    nc = tc.nc

    with ExitStack() as ctx:
        sb = ctx.enter_context(tc.tile_pool(name="sb", bufs=1))
        psum = ctx.enter_context(tc.psum_pool(name="psum", bufs=1))
        ctx.enter_context(tc.manual_schedule())

        words = {w: sb.tile([P, 2 * M], U8, name=w + "_words", align_bytes=64) for w in ("w1", "w2", "wo")}
        all_scales = sb.tile([P, 3 * M], U8, align_bytes=64)
        scale_column = {"w1": 0, "w2": M, "wo": 2 * M}
        tp_rows = sb.tile([P, P], F32, align_bytes=64)
        tp_cols = sb.tile([P, P], F32, align_bytes=64)
        half_tp = sb.tile([P, TILES], F32)
        minus_half_tp = sb.tile([P, TILES], F32)
        warm = sb.tile([P, 1], F32)
        raw = {a: sb.tile([P, PACK, N], F32, name=a + "_raw") for a in ("x", "dy")}
        grouped = {
            (a, first): sb.tile([P, last - first, PACK], BF16, name="%s_grouped%d" % (a, first), align_bytes=64)
            for a in ("x", "dy")
            for first, last in PIECES
        }
        codes = {a: sb.tile([P, N], U32, name=a + "_codes", align_bytes=64) for a in ("x", "dy")}
        code_scales = {a: sb.tile([P, N], U8, name=a + "_code_scales", align_bytes=64) for a in ("x", "dy")}
        old_sb = [sb.tile([P, N], F32, name="old%d" % i) for i in range(TILES)]
        tanh_sb = [sb.tile([P, N], F32, name="tanh%d" % i) for i in range(TILES)]
        exp_sb = [sb.tile([P, N], F32, name="exp%d" % i) for i in range(TILES)]
        gated = [sb.tile([P, N], F32, name="gated%d" % i) for i in range(TILES)]
        partial = [sb.tile([P, N], F32, name="partial%d" % i) for i in range(TILES)]
        result = [sb.tile([P, N], F32, name="result%d" % i) for i in range(TILES)]
        scaled_gate = sb.tile([P, N], F32)
        exp_sums = sb.tile([P, TILES], F32)
        gated_sums = {i: sb.tile([P, 1], F32, name="gated_sums%d" % i) for i in ORDER[:2]}
        inverses = sb.tile([P, TILES], F32)
        numerators = [sb.tile([P, 1], F32, name="numerators%d" % i) for i in range(TILES)]
        shares = [sb.tile([P, 1], F32, name="shares%d" % i) for i in range(TILES)]
        banks = [[psum.tile([P, N], F32, name="bank%d_%d" % (g, b)) for b in range(4)] for g in range(G)]
        z2_bank = [banks[i // HALVES][(0, 1)[i % HALVES]] for i in range(TILES)]
        z1_bank = [banks[i // HALVES][(3, 1)[i % HALVES]] for i in range(TILES)]
        c0_bank = [banks[i // HALVES][(2, 0)[i % HALVES]] for i in range(TILES)]

        def load_words(w, source):
            nc.sync.dma_start(
                out=words[w][:].bitcast(I32), in_=source.rearrange("g p b -> (g p) b").bitcast(I32)
            )

        def load_scales(w, source, quadrants):
            rows = source.rearrange("g f m -> (g f) m")
            for q in quadrants:
                nc.sync.dma_start(
                    out=all_scales[QUAD * q : QUAD * q + SCALE_ROWS, scale_column[w] : scale_column[w] + M].bitcast(I32),
                    in_=rows[SCALE_ROWS * q : SCALE_ROWS * (q + 1), :].bitcast(I32),
                )

        def load_operand(a, source):
            nc.sync.dma_start(out=raw[a][:], in_=source.rearrange("g (p j) n -> (g p) j n", j=PACK))

        def rows_of(tensor, i):
            g, t = divmod(i, HALVES)
            return tensor[g, t * P : (t + 1) * P, :]

        def load_old(i):
            nc.sync.dma_start(out=old_sb[i][:], in_=rows_of(old, i))

        def interleave(copy, a, piece, first, last):
            start = PIECES[piece][0]
            copy(
                out=grouped[a, start][:, first - start : last - start, :].rearrange("p (c i) j -> p c j i", i=4),
                in_=raw[a][:, :, first:last].rearrange("p j (c i) -> p c j i", i=4),
            )

        def interleave_all(a):
            for columns in VECTOR_COPIES:
                interleave(nc.vector.tensor_copy, a, *columns)
            for columns in SCALAR_COPIES:
                interleave(nc.scalar.copy, a, *columns)

        def quantize(a, first, last):
            nc.vector.quantize_mx(
                out=codes[a][:, first:last].bitcast(FP8X4),
                scales=code_scales[a][:, first:last],
                in_=grouped[a, first][:].rearrange("p n j -> p (n j)"),
            )

        def product(bank, w, a, i):
            g, t = divmod(i, HALVES)
            rows = slice(g * ROWS, (g + 1) * ROWS)
            column = scale_column[w] + P * t
            nc.tensor.matmul_mx(
                out=bank[i][:],
                lhsT=words[w][rows, 2 * P * t : 2 * P * (t + 1)].bitcast(FP4X4),
                lhsT_scale=all_scales[rows, column : column + P],
                rhs=codes[a][rows, :].bitcast(FP8X4),
                rhs_scale=code_scales[a][rows, :],
                start=True,
                stop=True,
            )

        def tanh_half(i):
            nc.scalar.activation(out=tanh_sb[i][:], in_=z2_bank[i][:], func=ACT.Tanh, scale=0.5)

        def exponential(i):
            nc.scalar.activation(
                out=exp_sb[i][:],
                in_=z1_bank[i][:],
                func=ACT.Exp,
                scale=tp_cols[:, QUAD * i : QUAD * i + 1],
                accum_out=exp_sums[:, i : i + 1],
            )

        def gate_scaled(i):
            nc.vector.scalar_tensor_tensor(
                out=gated[i][:],
                in0=c0_bank[i][:],
                scalar=1.0,
                in1=scaled_gate[:],
                op0=ALU.mult,
                op1=ALU.mult,
                accum_out=gated_sums[i][:],
            )

        def gate(i, row_sum):
            nc.vector.scalar_tensor_tensor(
                out=gated[i][:],
                in0=tanh_sb[i][:],
                scalar=1.0,
                in1=c0_bank[i][:],
                op0=ALU.add,
                op1=ALU.mult,
                accum_out=row_sum,
            )

        def add_old(i):
            nc.vector.scalar_tensor_tensor(
                out=partial[i][:],
                in0=gated[i][:],
                scalar=half_tp[:, i : i + 1],
                in1=old_sb[i][:],
                op0=ALU.mult,
                op1=ALU.add,
            )

        def finish(i):
            nc.vector.scalar_tensor_tensor(
                out=result[i][:],
                in0=exp_sb[i][:],
                scalar=shares[i][:],
                in1=partial[i][:],
                op0=ALU.mult,
                op1=ALU.add,
            )
            nc.sync.dma_start(out=rows_of(out, i), in_=result[i][:])

        def numerator(i):
            factor = -1.0 if i == ORDER[0] else minus_half_tp[:, i : i + 1]
            multiply(numerators[i][:], gated_sums[i][:], factor)

        def summed_numerator(i):
            nc.scalar.activation(
                out=tanh_sb[i][:],
                in_=gated[i][:],
                func=ACT.Copy,
                scale=minus_half_tp[:, i : i + 1],
                accum_out=numerators[i][:],
            )

        def share(i):
            multiply(shares[i][:], numerators[i][:], inverses[:, i : i + 1])

        def multiply(target, source, factor):
            nc.scalar.activation(out=target, in_=source, func=ACT.Copy, scale=factor)

        nc.vector.memset(all_scales[:].bitcast(I32), 0)
        nc.gpsimd.memset(tp_rows[:], 0.0)
        nc.gpsimd.dma_start(
            out=tp_rows[0:P:QUAD, :].rearrange("q (c i) -> q c i", i=QUAD),
            in_=tp.rearrange("g (t q i) o -> q (g t) (i o)", t=HALVES, i=QUAD),
        )
        a, b, c, d = ORDER
        load_operand("x", x)
        load_words("w2", w2_words)
        load_scales("w2", w2_scales, range(4))
        load_operand("dy", dy)
        load_words("wo", wo_words)
        load_scales("wo", wo_scales, range(4))
        load_words("w1", w1_words)
        load_scales("w1", w1_scales, range(1))
        load_old(a)
        load_scales("w1", w1_scales, range(1, 4))
        for i in (b, c, d):
            load_old(i)
        nc.vector.memset(warm[:], 0.0)
        nc.scalar.activation(out=warm[:], in_=warm[:], func=ACT.Exp)

        interleave_all("x")
        for piece in PIECES:
            quantize("x", *piece)
        for i in ORDER:
            product(z2_bank, "w2", "x", i)
        nc.vector.transpose(out=tp_cols[:], in_=tp_rows[:])
        nc.vector.tensor_scalar(
            out=half_tp[:], in0=tp_cols[:, 0:P:QUAD], scalar1=0.5, scalar2=None, op0=ALU.mult
        )
        interleave_all("dy")
        for piece in PIECES:
            quantize("dy", *piece)
        product(c0_bank, "wo", "dy", a)
        product(c0_bank, "wo", "dy", b)
        for i in ORDER:
            tanh_half(i)
        product(c0_bank, "wo", "dy", c)
        product(c0_bank, "wo", "dy", d)
        for i in ORDER:
            product(z1_bank, "w1", "x", i)
        nc.vector.tensor_scalar(
            out=scaled_gate[:],
            in0=tanh_sb[a][:],
            scalar1=half_tp[:, a : a + 1],
            scalar2=half_tp[:, a : a + 1],
            op0=ALU.mult,
            op1=ALU.add,
        )
        multiply(minus_half_tp[:], tp_cols[:, 0:P:QUAD], -0.5)
        for i in ORDER:
            exponential(i)
        gate_scaled(a)
        nc.gpsimd.tensor_tensor(out=partial[a][:], in0=gated[a][:], in1=old_sb[a][:], op=ALU.add)
        gate(b, gated_sums[b][:])
        gate(c, None)
        gate(d, None)
        add_old(b)
        add_old(c)
        nc.vector.reciprocal(out=inverses[:], in_=exp_sums[:])
        add_old(d)
        numerator(a)
        numerator(b)
        summed_numerator(c)
        share(a)
        share(b)
        summed_numerator(d)
        share(c)
        share(d)
        for i in ORDER:
            finish(i)
